import numpy as np
import ml_dtypes


def mxq(x, axis, fmt="e4m3"):
    dtype, down = {"e4m3": (ml_dtypes.float8_e4m3fn, 7), "e5m2": (ml_dtypes.float8_e5m2, 14)}[fmt]
    v = np.moveaxis(np.asarray(x, np.float32).astype(ml_dtypes.bfloat16).astype(np.float64), axis, -1)
    blocks = v.reshape(v.shape[:-1] + (-1, 32))
    amax = np.abs(blocks).max(-1, keepdims=True)
    byte = np.maximum(np.where(amax > 0, np.frexp(amax)[1] - 1 + 127, 0) - down, 1)
    scale = np.exp2(byte - 127.0)
    codes = (blocks / scale).astype(np.float32).astype(dtype).astype(np.float64)
    return np.moveaxis((codes * scale).reshape(v.shape), -1, axis)


WIDE = False


def mx_kscale(k):
    if not WIDE:
        return np.ones(k)
    levels = np.array([10, -10, 5, -5, 0])
    if k % 512:
        return np.exp2(np.random.permutation(np.resize(levels, k // 32))).repeat(32)
    a = np.empty((k // 512, 16))
    for p in range(k // 512):
        a[p, :8] = np.random.permutation(np.resize(levels, 8))
        for g in range(8):
            far = levels[np.abs(levels - a[p, g]) >= 10]
            a[p, g + 8] = far[np.random.randint(len(far))]
    return np.exp2(a.ravel()).repeat(32)


def f64(x):
    return np.asarray(x).astype(np.float64)


def striped(idx):
    return np.tile(np.asarray(idx).reshape(-1, 16).T, (8, 1)).astype(np.uint16)


def unstriped(offs):
    return offs[:16].T.reshape(-1).astype(np.int64)


E2M1 = np.array([0.0, 0.5, 1.0, 1.5, 2.0, 3.0, 4.0, 6.0, -0.0, -0.5, -1.0, -1.5, -2.0, -3.0, -4.0, -6.0])


def pack_weight(w, fmt):
    k, n = w.shape
    w = f64(np.asarray(w, np.float32).astype(ml_dtypes.bfloat16)).reshape(k // 32, 32, n)
    amax = np.abs(w).max(1)
    if fmt == "e4m3":
        byte = np.frexp(amax)[1] - 1 + 127 - 7
    else:
        mant, ex = np.frexp(amax / 6.0)
        byte = np.where(mant > 0.5, ex, ex - 1) + 127
    byte = np.clip(np.where(amax > 0, byte, 1), 1, 254)
    scaled = (w * np.exp2(127.0 - byte)[:, None, :]).reshape(k, n).astype(np.float32)
    by_word = np.ascontiguousarray(scaled.reshape(k // 512, 128, 4, n).transpose(0, 1, 3, 2))
    if fmt == "e4m3":
        words = by_word.astype(ml_dtypes.float8_e4m3fn).view(np.uint8)
    else:
        c = by_word.astype(ml_dtypes.float4_e2m1fn).view(np.uint8) & 0xF
        words = (c[..., 0::2] | (c[..., 1::2] << 4)).reshape(k // 512, 128, 2 * n)
    return np.ascontiguousarray(words), np.ascontiguousarray(byte.astype(np.uint8).reshape(k // 512, 16, n))


def unpack_weight(words, scales, fmt):
    g, _, n = scales.shape
    words = np.ascontiguousarray(words).reshape(g, 128, n, -1)
    if fmt == "e4m3":
        vals = words.view(ml_dtypes.float8_e4m3fn).astype(np.float64)
    else:
        nib = np.empty((g, 128, n, 4), np.uint8)
        nib[..., 0::2] = words & 0xF
        nib[..., 1::2] = words >> 4
        vals = E2M1[nib]
    vals = vals * np.repeat(np.exp2(scales.astype(np.float64) - 127.0), 8, axis=1)[..., None]
    return vals.transpose(0, 1, 3, 2).reshape(g * 512, n)


def bf(x):
    return np.asarray(x, np.float32).astype(ml_dtypes.bfloat16)


def planes(Y):
    r, m = Y.shape
    b = f64(bf(Y)).reshape(r // 32, 32, m)
    amax = np.abs(b).max(1)
    byte = np.clip(np.where(amax > 0, np.frexp(amax)[1] - 1 + 127 - 7, 1), 1, 254)
    codes = (b * np.exp2(127.0 - byte)[:, None, :]).reshape(r, m).astype(np.float32).astype(ml_dtypes.float8_e4m3fn).view(np.uint8)
    words = codes.reshape(r // 512, 128, 4, m).transpose(0, 1, 3, 2)
    return np.ascontiguousarray(words), np.ascontiguousarray(byte.astype(np.uint8).reshape(r // 512, 16, m))


D, T, I, Q, E, U = 512, 2048, 512, 256, 512, 1024


def setup_inputs():
    n = np.random.standard_normal
    idx = np.random.permutation(T)[:I]
    idx2 = np.random.permutation(U)[:Q]
    idx3 = np.random.permutation(U)[:Q]
    fd = mx_kscale(D)
    fi = mx_kscale(I)
    ti = np.ones(T)
    ti[idx] = fi
    keysp = pack_weight(n((D, T)) / fd[:, None], "e2m1")
    return {
        "users": (n((D, U)) * 1.0 / np.sqrt(D) * fd[:, None]).astype(np.float32),
        "keys_words": keysp[0],
        "keys_scales": keysp[1],
        "os": (np.random.uniform(0.02, 0.08, (1, I)) * fi).astype(np.float32),
        "vals": (n((E, T)) / ti).astype(np.float32),
        "offs": striped(idx),
        "offs2": striped(idx2),
        "offs3": striped(idx3),
    }


def reference(users, keys_words, keys_scales, os, vals, offs, offs2, offs3):
    idx = unstriped(offs)
    idx2 = unstriped(offs2)
    idx3 = unstriped(offs3)
    keysu = unpack_weight(keys_words, keys_scales, "e2m1")
    zq = np.maximum(f64(users)[:, idx2], f64(users)[:, idx3])
    zqq = mxq(zq, 0, "e4m3")
    keysidxg = keysu[:, idx]
    s = zqq.T @ keysidxg
    w = np.maximum(s, 0.0)
    wo1 = w * f64(os)
    wt1 = wo1.T
    vt1 = f64(vals)[:, idx].T
    vt1q = mxq(vt1, 0, "e4m3")
    wt1q = mxq(wt1, 0, "e4m3")
    o = vt1q.T @ wt1q
    words, scales = planes(o)
    return o, words, scales

@@ -1,0 +1,184 @@
+from contextlib import ExitStack
+
+import concourse.mybir as mybir
+from concourse.masks import make_identity
+
+D, T, I, Q, E, U = 512, 2048, 512, 256, 512, 1024
+FLOPS = 2 * Q * I * D + 2 * E * Q * I
+
+F32 = mybir.dt.float32
+BF16 = mybir.dt.bfloat16
+I32 = mybir.dt.int32
+U32 = mybir.dt.uint32
+U16 = mybir.dt.uint16
+U8 = mybir.dt.uint8
+FP8X4 = mybir.dt.float8_e4m3fn_x4
+FP4X4 = mybir.dt.float4_e2m1fn_x4
+ALU = mybir.AluOpType
+COPY = mybir.ActivationFunctionType.Copy
+
+P = 128
+PACK = 4
+HALF = Q // 2
+QUADS = 4
+LIST_ROWS = 16
+SPLIT = 288
+
+
+def tile_attend_querylarger_read_lean_pl_kernel(
+    tc, users, keys_words, keys_scales, slot_factor, vals, offs, offs2, offs3, out_0, out_1, out_2
+):
+    nc = tc.nc
+    with ExitStack() as ctx:
+        keep = ctx.enter_context(tc.tile_pool(name="keep", bufs=1))
+        psum = ctx.enter_context(tc.psum_pool(name="psum", bufs=1))
+
+        slots = keep.tile([P, I // LIST_ROWS], U16, name="slots")
+        first = keep.tile([P, Q // LIST_ROWS], U16, name="first")
+        second = keep.tile([P, Q // LIST_ROWS], U16, name="second")
+        user_rows = [keep.tile([P, U], F32, name="user_rows%d" % t) for t in range(PACK)]
+        val_rows = [keep.tile([P, T], F32, name="val_rows%d" % t, tag="val_rows%d" % t, align_bytes=64) for t in range(PACK)]
+        key_words = keep.tile([P, T], U16, name="key_words")
+        key_scales = keep.tile([P, T], U8, name="key_scales")
+        factor = keep.tile([P, PACK], F32, name="factor")
+        ident = keep.tile([P, P], F32, name="ident")
+
+        nc.gpsimd.memset(key_scales[:].bitcast(I32), 0)
+        make_identity(nc, ident[:])
+
+        users_by_place = users.rearrange("(p t) u -> t p u", t=PACK)
+        vals_by_place = vals.rearrange("(p t) c -> t p c", t=PACK)
+        out_by_pair = out_0.rearrange("(p a t) q -> a p t q", a=2, t=2)
+
+        nc.sync.dma_start(user_rows[0][:], users_by_place[0])
+        nc.sync.dma_start(first[:], offs2)
+        nc.sync.dma_start(second[:], offs3)
+        nc.sync.dma_start(user_rows[1][:], users_by_place[1])
+        for g in range(QUADS):
+            nc.sync.dma_start(
+                key_scales[32 * g : 32 * g + 4, :].bitcast(I32), keys_scales[0, 4 * g : 4 * g + 4, :].bitcast(I32)
+            )
+        nc.sync.dma_start(slots[:], offs)
+        nc.sync.dma_start(key_words[:].bitcast(I32), keys_words[0].bitcast(I32))
+        for t in range(2, PACK):
+            nc.sync.dma_start(user_rows[t][:], users_by_place[t])
+        nc.sync.dma_start(factor[:], slot_factor.rearrange("o (p r) -> p (o r)", r=PACK))
+        for t in range(PACK):
+            nc.sync.dma_start(val_rows[t][:], vals_by_place[t])
+
+        first_cols = keep.tile([P, PACK, Q], F32, name="first_cols")
+        second_cols = keep.tile([P, PACK, Q], F32, name="second_cols")
+        for t in range(PACK):
+            nc.vector.tensor_copy(first_cols[:, t, :], user_rows[t][:].indirect(first[:]))
+            nc.scalar.activation(second_cols[:, t, :], user_rows[t][:].indirect(second[:]), COPY)
+        zq = keep.tile([P, Q * PACK], BF16, name="zq", align_bytes=64)
+        nc.vector.tensor_tensor(
+            zq[:].rearrange("p (c j t) -> p c t j", j=4, t=PACK),
+            first_cols[:].rearrange("p t (c j) -> p c t j", j=4),
+            second_cols[:].rearrange("p t (c j) -> p c t j", j=4),
+            ALU.max,
+        )
+        zq_codes = keep.tile([P, Q], U32, name="zq_codes", align_bytes=64)
+        zq_scales = keep.tile([P, Q], U8, name="zq_scales", align_bytes=64)
+        nc.vector.quantize_mx(zq_codes[:].bitcast(FP8X4), zq_scales[:], zq[:])
+
+        listed_words = keep.tile([P, I], U16, name="listed_words")
+        dealt_words = keep.tile([P, I], U16, name="dealt_words", align_bytes=64)
+        dealt_scales = keep.tile([P, I], U8, name="dealt_scales", align_bytes=64)
+        nc.vector.tensor_copy(listed_words[:], key_words[:].indirect(slots[:]))
+        nc.vector.tensor_copy(dealt_scales[:].rearrange("p (r s) -> p s r", r=PACK), key_scales[:].indirect(slots[:]))
+        nc.vector.tensor_copy(
+            dealt_words[:].rearrange("p (r s) -> p r s", r=PACK), listed_words[:].rearrange("p (s r) -> p r s", r=PACK)
+        )
+
+        w_codes = keep.tile([P, Q], U32, name="w_codes", align_bytes=64)
+        w_scales = keep.tile([P, Q], U8, name="w_scales", align_bytes=64)
+        weights = keep.tile([P, Q * PACK], BF16, name="weights", align_bytes=64)
+        for h in range(2):
+            q_cols = slice(h * HALF, (h + 1) * HALF)
+            scores = psum.tile([P, PACK, HALF], F32, name="scores%d" % h)
+            for r in range(PACK):
+                nc.tensor.matmul_mx(
+                    scores[:, r, :],
+                    lhsT=dealt_words[:, r * P : (r + 1) * P].bitcast(FP4X4),
+                    lhsT_scale=dealt_scales[:, r * P : (r + 1) * P],
+                    rhs=zq_codes[:, q_cols].bitcast(FP8X4),
+                    rhs_scale=zq_scales[:, q_cols],
+                    start=True,
+                    stop=True,
+                )
+            nc.vector.scalar_tensor_tensor(
+                weights[:, h * HALF * PACK : (h + 1) * HALF * PACK].rearrange("p (q r) -> p q r", r=PACK),
+                scores[:].rearrange("p r q -> p q r"),
+                0.0,
+                factor[:].unsqueeze(1).to_broadcast([P, HALF, PACK]),
+                ALU.max,
+                ALU.mult,
+            )
+        nc.vector.quantize_mx(w_codes[:].bitcast(FP8X4), w_scales[:], weights[:])
+
+        sums = [psum.tile([P, PACK, HALF], F32, name="sums%d" % h) for h in range(2)]
+        rounded = keep.tile([P, Q * PACK], BF16, name="rounded", align_bytes=64)
+        out_codes = keep.tile([P, Q], U32, name="out_codes", align_bytes=64)
+        out_scales = keep.tile([P, Q], U8, name="out_scales", align_bytes=64)
+        listed = [keep.tile([P, I], BF16, name="listed%d" % t) for t in range(PACK)]
+        for t in range(PACK - 1):
+            nc.scalar.activation(listed[t][:], val_rows[t][:].indirect(slots[:]), COPY)
+        nc.vector.tensor_copy(listed[-1][:, :SPLIT], val_rows[-1][:].indirect(slots[:, : SPLIT // LIST_ROWS]))
+        nc.scalar.activation(listed[-1][:, SPLIT:], val_rows[-1][:].indirect(slots[:, SPLIT // LIST_ROWS :]), COPY)
+        held = keep.tile([P, 2 * P + 2 * Q], F32, name="held", tag="val_rows%d" % (PACK - 1), align_bytes=64)
+
+        for t in range(PACK):
+            pairs = listed[t][:].bitcast(F32)
+            turned = psum.tile([P, 2, P], F32, name="turned%d" % t)
+            for u in range(2):
+                nc.tensor.transpose(turned[:, u, :], pairs[:, u : I // 2 : 2], ident[:])
+            if t == PACK - 2:
+                grouped = held[:, : 2 * P]
+            else:
+                grouped = keep.tile([P, 2 * P], F32, name="grouped%d" % t, align_bytes=64)[:]
+            (nc.scalar.copy if t == PACK - 1 else nc.vector.tensor_copy)(
+                grouped.rearrange("p (m u) -> p m u", u=2), turned[:].rearrange("p u m -> p m u")
+            )
+            v_codes = keep.tile([P, P], U32, name="v_codes%d" % t, align_bytes=64)
+            v_scales = keep.tile([P, P], U8, name="v_scales%d" % t, align_bytes=64)
+            nc.vector.quantize_mx(v_codes[:].bitcast(FP8X4), v_scales[:], grouped.bitcast(BF16))
+            for h in range(2):
+                q_cols = slice(h * HALF, (h + 1) * HALF)
+                nc.tensor.matmul_mx(
+                    sums[h][:, t, :],
+                    lhsT=v_codes[:].bitcast(FP8X4),
+                    lhsT_scale=v_scales[:],
+                    rhs=w_codes[:, q_cols].bitcast(FP8X4),
+                    rhs_scale=w_scales[:, q_cols],
+                    start=True,
+                    stop=True,
+                )
+            if t == 1:
+                early = held[:, 2 * P :].rearrange("p (t q) -> p t q", t=2)
+                for h in range(2):
+                    nc.scalar.copy(early[:, :, h * HALF : (h + 1) * HALF], sums[h][:, :2, :])
+                nc.sync.dma_start(out_by_pair[0], early)
+
+        for h, engine_copy in ((1, nc.scalar.copy), (0, nc.vector.tensor_copy)):
+            engine_copy(
+                rounded[:, h * HALF * PACK : (h + 1) * HALF * PACK].rearrange("p (q t) -> p q t", t=PACK),
+                sums[h][:].rearrange("p t q -> p q t"),
+            )
+        for h in (1, 0):
+            q_cols = slice(h * HALF, (h + 1) * HALF)
+            nc.vector.quantize_mx(
+                out_codes[:, q_cols].bitcast(FP8X4),
+                out_scales[:, q_cols],
+                rounded[:, h * HALF * PACK : (h + 1) * HALF * PACK],
+            )
+        late = keep.tile([P, 2, Q], F32, name="late")
+        for h in (1, 0):
+            nc.scalar.copy(late[:, :, h * HALF : (h + 1) * HALF], sums[h][:, 2:, :])
+        nc.scalar.dma_start(out_by_pair[1], late[:])
+
+        nc.sync.dma_start(out_1[0].rearrange("p q t -> p (q t)").bitcast(I32), out_codes[:].bitcast(I32))
+        for g in range(QUADS):
+            (nc.sync if g < 2 else nc.scalar).dma_start(
+                out_2[0, 4 * g : 4 * g + 4, :].bitcast(I32), out_scales[32 * g : 32 * g + 4, :].bitcast(I32)
+            )

@@ -43,44 +43,27 @@ def tile_attend_querylarger_read_lean_pl_kernel(
         factor = keep.tile([P, PACK], F32, name="factor")
         ident = keep.tile([P, P], F32, name="ident")
 
-        nc.gpsimd.memset(key_scales[:].bitcast(I32), 0)
+        nc.vector.memset(key_scales[:].bitcast(I32), 0)
         make_identity(nc, ident[:])
 
         users_by_place = users.rearrange("(p t) u -> t p u", t=PACK)
         vals_by_place = vals.rearrange("(p t) c -> t p c", t=PACK)
         out_by_pair = out_0.rearrange("(p a t) q -> a p t q", a=2, t=2)
 
-        nc.sync.dma_start(user_rows[0][:], users_by_place[0])
+        nc.scalar.dma_start(user_rows[0][:], users_by_place[0])
         nc.sync.dma_start(first[:], offs2)
         nc.sync.dma_start(second[:], offs3)
-        nc.sync.dma_start(user_rows[1][:], users_by_place[1])
+        nc.sync.dma_start(slots[:], offs)
+        nc.sync.dma_start(key_words[:].bitcast(I32), keys_words[0].bitcast(I32))
         for g in range(QUADS):
             nc.sync.dma_start(
                 key_scales[32 * g : 32 * g + 4, :].bitcast(I32), keys_scales[0, 4 * g : 4 * g + 4, :].bitcast(I32)
             )
-        nc.sync.dma_start(slots[:], offs)
-        nc.sync.dma_start(key_words[:].bitcast(I32), keys_words[0].bitcast(I32))
-        for t in range(2, PACK):
+        for t in range(1, PACK):
             nc.sync.dma_start(user_rows[t][:], users_by_place[t])
         nc.sync.dma_start(factor[:], slot_factor.rearrange("o (p r) -> p (o r)", r=PACK))
         for t in range(PACK):
             nc.sync.dma_start(val_rows[t][:], vals_by_place[t])
-
-        first_cols = keep.tile([P, PACK, Q], F32, name="first_cols")
-        second_cols = keep.tile([P, PACK, Q], F32, name="second_cols")
-        for t in range(PACK):
-            nc.vector.tensor_copy(first_cols[:, t, :], user_rows[t][:].indirect(first[:]))
-            nc.scalar.activation(second_cols[:, t, :], user_rows[t][:].indirect(second[:]), COPY)
-        zq = keep.tile([P, Q * PACK], BF16, name="zq", align_bytes=64)
-        nc.vector.tensor_tensor(
-            zq[:].rearrange("p (c j t) -> p c t j", j=4, t=PACK),
-            first_cols[:].rearrange("p t (c j) -> p c t j", j=4),
-            second_cols[:].rearrange("p t (c j) -> p c t j", j=4),
-            ALU.max,
-        )
-        zq_codes = keep.tile([P, Q], U32, name="zq_codes", align_bytes=64)
-        zq_scales = keep.tile([P, Q], U8, name="zq_scales", align_bytes=64)
-        nc.vector.quantize_mx(zq_codes[:].bitcast(FP8X4), zq_scales[:], zq[:])
 
         listed_words = keep.tile([P, I], U16, name="listed_words")
         dealt_words = keep.tile([P, I], U16, name="dealt_words", align_bytes=64)
@@ -91,12 +74,34 @@ def tile_attend_querylarger_read_lean_pl_kernel(
             dealt_words[:].rearrange("p (r s) -> p r s", r=PACK), listed_words[:].rearrange("p (s r) -> p r s", r=PACK)
         )
 
+        first_cols = keep.tile([P, PACK, Q], F32, name="first_cols")
+        second_cols = keep.tile([P, PACK, Q], F32, name="second_cols")
+        for t in range(PACK):
+            if t == 0:
+                nc.scalar.activation(first_cols[:, t, :], user_rows[t][:].indirect(first[:]), COPY)
+            else:
+                nc.vector.tensor_copy(first_cols[:, t, :], user_rows[t][:].indirect(first[:]))
+            nc.scalar.activation(second_cols[:, t, :], user_rows[t][:].indirect(second[:]), COPY)
+        zq = keep.tile([P, Q * PACK], BF16, name="zq", align_bytes=64)
+        zq_codes = keep.tile([P, Q], U32, name="zq_codes", align_bytes=64)
+        zq_scales = keep.tile([P, Q], U8, name="zq_scales", align_bytes=64)
+        for h in range(2):
+            q_cols = slice(h * HALF, (h + 1) * HALF)
+            words = slice(h * HALF * PACK, (h + 1) * HALF * PACK)
+            nc.vector.tensor_tensor(
+                zq[:, words].rearrange("p (c j t) -> p c t j", j=4, t=PACK),
+                first_cols[:, :, q_cols].rearrange("p t (c j) -> p c t j", j=4),
+                second_cols[:, :, q_cols].rearrange("p t (c j) -> p c t j", j=4),
+                ALU.max,
+            )
+            nc.vector.quantize_mx(zq_codes[:, q_cols].bitcast(FP8X4), zq_scales[:, q_cols], zq[:, words])
+
         w_codes = keep.tile([P, Q], U32, name="w_codes", align_bytes=64)
         w_scales = keep.tile([P, Q], U8, name="w_scales", align_bytes=64)
         weights = keep.tile([P, Q * PACK], BF16, name="weights", align_bytes=64)
         for h in range(2):
             q_cols = slice(h * HALF, (h + 1) * HALF)
-            scores = psum.tile([P, PACK, HALF], F32, name="scores%d" % h)
+            scores = psum.tile([P, PACK, HALF], F32, name="scores%d" % h, tag="bank%d" % h)
             for r in range(PACK):
                 nc.tensor.matmul_mx(
                     scores[:, r, :],
@@ -130,7 +135,7 @@ def tile_attend_querylarger_read_lean_pl_kernel(
 
         for t in range(PACK):
             pairs = listed[t][:].bitcast(F32)
-            turned = psum.tile([P, 2, P], F32, name="turned%d" % t)
+            turned = psum.tile([P, 2, P], F32, name="turned%d" % t, tag="bank%d" % t)
             for u in range(2):
                 nc.tensor.transpose(turned[:, u, :], pairs[:, u : I // 2 : 2], ident[:])
             if t == PACK - 2:

@@ -22,7 +22,7 @@ PACK = 4
 HALF = Q // 2
 QUADS = 4
 LIST_ROWS = 16
-SPLIT = 288
+SPLIT = 256
 
 
 def tile_attend_querylarger_read_lean_pl_kernel(
@@ -50,11 +50,11 @@ def tile_attend_querylarger_read_lean_pl_kernel(
         vals_by_place = vals.rearrange("(p t) c -> t p c", t=PACK)
         out_by_pair = out_0.rearrange("(p a t) q -> a p t q", a=2, t=2)
 
-        nc.scalar.dma_start(user_rows[0][:], users_by_place[0])
+        nc.scalar.dma_start(key_words[:].bitcast(I32), keys_words[0].bitcast(I32))
         nc.sync.dma_start(first[:], offs2)
         nc.sync.dma_start(second[:], offs3)
         nc.sync.dma_start(slots[:], offs)
-        nc.sync.dma_start(key_words[:].bitcast(I32), keys_words[0].bitcast(I32))
+        nc.sync.dma_start(user_rows[0][:], users_by_place[0])
         for g in range(QUADS):
             nc.sync.dma_start(
                 key_scales[32 * g : 32 * g + 4, :].bitcast(I32), keys_scales[0, 4 * g : 4 * g + 4, :].bitcast(I32)
@@ -66,21 +66,20 @@ def tile_attend_querylarger_read_lean_pl_kernel(
             nc.sync.dma_start(val_rows[t][:], vals_by_place[t])
 
         listed_words = keep.tile([P, I], U16, name="listed_words")
+        listed_scales = keep.tile([P, I], U8, name="listed_scales")
         dealt_words = keep.tile([P, I], U16, name="dealt_words", align_bytes=64)
         dealt_scales = keep.tile([P, I], U8, name="dealt_scales", align_bytes=64)
         nc.vector.tensor_copy(listed_words[:], key_words[:].indirect(slots[:]))
-        nc.vector.tensor_copy(dealt_scales[:].rearrange("p (r s) -> p s r", r=PACK), key_scales[:].indirect(slots[:]))
-        nc.vector.tensor_copy(
-            dealt_words[:].rearrange("p (r s) -> p r s", r=PACK), listed_words[:].rearrange("p (s r) -> p r s", r=PACK)
-        )
+        nc.vector.tensor_copy(listed_scales[:], key_scales[:].indirect(slots[:]))
+        for dealt, gathered in ((dealt_words, listed_words), (dealt_scales, listed_scales)):
+            nc.vector.tensor_copy(
+                dealt[:].rearrange("p (r s) -> p r s", r=PACK), gathered[:].rearrange("p (s r) -> p r s", r=PACK)
+            )
 
         first_cols = keep.tile([P, PACK, Q], F32, name="first_cols")
         second_cols = keep.tile([P, PACK, Q], F32, name="second_cols")
         for t in range(PACK):
-            if t == 0:
-                nc.scalar.activation(first_cols[:, t, :], user_rows[t][:].indirect(first[:]), COPY)
-            else:
-                nc.vector.tensor_copy(first_cols[:, t, :], user_rows[t][:].indirect(first[:]))
+            nc.vector.tensor_copy(first_cols[:, t, :], user_rows[t][:].indirect(first[:]))
             nc.scalar.activation(second_cols[:, t, :], user_rows[t][:].indirect(second[:]), COPY)
         zq = keep.tile([P, Q * PACK], BF16, name="zq", align_bytes=64)
         zq_codes = keep.tile([P, Q], U32, name="zq_codes", align_bytes=64)
@@ -89,9 +88,9 @@ def tile_attend_querylarger_read_lean_pl_kernel(
             q_cols = slice(h * HALF, (h + 1) * HALF)
             words = slice(h * HALF * PACK, (h + 1) * HALF * PACK)
             nc.vector.tensor_tensor(
-                zq[:, words].rearrange("p (c j t) -> p c t j", j=4, t=PACK),
-                first_cols[:, :, q_cols].rearrange("p t (c j) -> p c t j", j=4),
-                second_cols[:, :, q_cols].rearrange("p t (c j) -> p c t j", j=4),
+                zq[:, words].rearrange("p (c j t) -> p c t j", j=2, t=PACK),
+                first_cols[:, :, q_cols].rearrange("p t (c j) -> p c t j", j=2),
+                second_cols[:, :, q_cols].rearrange("p t (c j) -> p c t j", j=2),
                 ALU.max,
             )
             nc.vector.quantize_mx(zq_codes[:, q_cols].bitcast(FP8X4), zq_scales[:, q_cols], zq[:, words])

from contextlib import ExitStack

import concourse.mybir as mybir
from concourse.masks import make_identity

D, T, I, Q, E, U = 512, 2048, 512, 256, 512, 1024
FLOPS = 2 * Q * I * D + 2 * E * Q * I

F32 = mybir.dt.float32
BF16 = mybir.dt.bfloat16
I32 = mybir.dt.int32
U32 = mybir.dt.uint32
U16 = mybir.dt.uint16
U8 = mybir.dt.uint8
FP8X4 = mybir.dt.float8_e4m3fn_x4
FP4X4 = mybir.dt.float4_e2m1fn_x4
ALU = mybir.AluOpType
COPY = mybir.ActivationFunctionType.Copy

P = 128
PACK = 4
HALF = Q // 2
QUADS = 4
LIST_ROWS = 16
SPLIT = 256


def tile_attend_querylarger_read_lean_pl_kernel(
    tc, users, keys_words, keys_scales, slot_factor, vals, offs, offs2, offs3, out_0, out_1, out_2
):
    nc = tc.nc
    with ExitStack() as ctx:
        keep = ctx.enter_context(tc.tile_pool(name="keep", bufs=1))
        psum = ctx.enter_context(tc.psum_pool(name="psum", bufs=1))

        slots = keep.tile([P, I // LIST_ROWS], U16, name="slots")
        first = keep.tile([P, Q // LIST_ROWS], U16, name="first")
        second = keep.tile([P, Q // LIST_ROWS], U16, name="second")
        user_rows = [keep.tile([P, U], F32, name="user_rows%d" % t) for t in range(PACK)]
        val_rows = [keep.tile([P, T], F32, name="val_rows%d" % t, tag="val_rows%d" % t, align_bytes=64) for t in range(PACK)]
        key_words = keep.tile([P, T], U16, name="key_words")
        key_scales = keep.tile([P, T], U8, name="key_scales")
        factor = keep.tile([P, PACK], F32, name="factor")
        ident = keep.tile([P, P], F32, name="ident")

        nc.vector.memset(key_scales[:].bitcast(I32), 0)
        make_identity(nc, ident[:])

        users_by_place = users.rearrange("(p t) u -> t p u", t=PACK)
        vals_by_place = vals.rearrange("(p t) c -> t p c", t=PACK)
        out_by_pair = out_0.rearrange("(p a t) q -> a p t q", a=2, t=2)

        nc.scalar.dma_start(key_words[:].bitcast(I32), keys_words[0].bitcast(I32))
        nc.sync.dma_start(first[:], offs2)
        nc.sync.dma_start(second[:], offs3)
        nc.sync.dma_start(slots[:], offs)
        nc.sync.dma_start(user_rows[0][:], users_by_place[0])
        for g in range(QUADS):
            nc.sync.dma_start(
                key_scales[32 * g : 32 * g + 4, :].bitcast(I32), keys_scales[0, 4 * g : 4 * g + 4, :].bitcast(I32)
            )
        for t in range(1, PACK):
            nc.sync.dma_start(user_rows[t][:], users_by_place[t])
        nc.sync.dma_start(factor[:], slot_factor.rearrange("o (p r) -> p (o r)", r=PACK))
        for t in range(PACK):
            nc.sync.dma_start(val_rows[t][:], vals_by_place[t])

        listed_words = keep.tile([P, I], U16, name="listed_words")
        listed_scales = keep.tile([P, I], U8, name="listed_scales")
        dealt_words = keep.tile([P, I], U16, name="dealt_words", align_bytes=64)
        dealt_scales = keep.tile([P, I], U8, name="dealt_scales", align_bytes=64)
        nc.vector.tensor_copy(listed_words[:], key_words[:].indirect(slots[:]))
        nc.vector.tensor_copy(listed_scales[:], key_scales[:].indirect(slots[:]))
        for dealt, gathered in ((dealt_words, listed_words), (dealt_scales, listed_scales)):
            nc.vector.tensor_copy(
                dealt[:].rearrange("p (r s) -> p r s", r=PACK), gathered[:].rearrange("p (s r) -> p r s", r=PACK)
            )

        first_cols = keep.tile([P, PACK, Q], F32, name="first_cols")
        second_cols = keep.tile([P, PACK, Q], F32, name="second_cols")
        for t in range(PACK):
            nc.vector.tensor_copy(first_cols[:, t, :], user_rows[t][:].indirect(first[:]))
            nc.scalar.activation(second_cols[:, t, :], user_rows[t][:].indirect(second[:]), COPY)
        zq = keep.tile([P, Q * PACK], BF16, name="zq", align_bytes=64)
        zq_codes = keep.tile([P, Q], U32, name="zq_codes", align_bytes=64)
        zq_scales = keep.tile([P, Q], U8, name="zq_scales", align_bytes=64)
        for h in range(2):
            q_cols = slice(h * HALF, (h + 1) * HALF)
            words = slice(h * HALF * PACK, (h + 1) * HALF * PACK)
            nc.vector.tensor_tensor(
                zq[:, words].rearrange("p (c j t) -> p c t j", j=2, t=PACK),
                first_cols[:, :, q_cols].rearrange("p t (c j) -> p c t j", j=2),
                second_cols[:, :, q_cols].rearrange("p t (c j) -> p c t j", j=2),
                ALU.max,
            )
            nc.vector.quantize_mx(zq_codes[:, q_cols].bitcast(FP8X4), zq_scales[:, q_cols], zq[:, words])

        w_codes = keep.tile([P, Q], U32, name="w_codes", align_bytes=64)
        w_scales = keep.tile([P, Q], U8, name="w_scales", align_bytes=64)
        weights = keep.tile([P, Q * PACK], BF16, name="weights", align_bytes=64)
        for h in range(2):
            q_cols = slice(h * HALF, (h + 1) * HALF)
            scores = psum.tile([P, PACK, HALF], F32, name="scores%d" % h, tag="bank%d" % h)
            for r in range(PACK):
                nc.tensor.matmul_mx(
                    scores[:, r, :],
                    lhsT=dealt_words[:, r * P : (r + 1) * P].bitcast(FP4X4),
                    lhsT_scale=dealt_scales[:, r * P : (r + 1) * P],
                    rhs=zq_codes[:, q_cols].bitcast(FP8X4),
                    rhs_scale=zq_scales[:, q_cols],
                    start=True,
                    stop=True,
                )
            nc.vector.scalar_tensor_tensor(
                weights[:, h * HALF * PACK : (h + 1) * HALF * PACK].rearrange("p (q r) -> p q r", r=PACK),
                scores[:].rearrange("p r q -> p q r"),
                0.0,
                factor[:].unsqueeze(1).to_broadcast([P, HALF, PACK]),
                ALU.max,
                ALU.mult,
            )
        nc.vector.quantize_mx(w_codes[:].bitcast(FP8X4), w_scales[:], weights[:])

        sums = [psum.tile([P, PACK, HALF], F32, name="sums%d" % h) for h in range(2)]
        rounded = keep.tile([P, Q * PACK], BF16, name="rounded", align_bytes=64)
        out_codes = keep.tile([P, Q], U32, name="out_codes", align_bytes=64)
        out_scales = keep.tile([P, Q], U8, name="out_scales", align_bytes=64)
        listed = [keep.tile([P, I], BF16, name="listed%d" % t) for t in range(PACK)]
        for t in range(PACK - 1):
            nc.scalar.activation(listed[t][:], val_rows[t][:].indirect(slots[:]), COPY)
        nc.vector.tensor_copy(listed[-1][:, :SPLIT], val_rows[-1][:].indirect(slots[:, : SPLIT // LIST_ROWS]))
        nc.scalar.activation(listed[-1][:, SPLIT:], val_rows[-1][:].indirect(slots[:, SPLIT // LIST_ROWS :]), COPY)
        held = keep.tile([P, 2 * P + 2 * Q], F32, name="held", tag="val_rows%d" % (PACK - 1), align_bytes=64)

        for t in range(PACK):
            pairs = listed[t][:].bitcast(F32)
            turned = psum.tile([P, 2, P], F32, name="turned%d" % t, tag="bank%d" % t)
            for u in range(2):
                nc.tensor.transpose(turned[:, u, :], pairs[:, u : I // 2 : 2], ident[:])
            if t == PACK - 2:
                grouped = held[:, : 2 * P]
            else:
                grouped = keep.tile([P, 2 * P], F32, name="grouped%d" % t, align_bytes=64)[:]
            (nc.scalar.copy if t == PACK - 1 else nc.vector.tensor_copy)(
                grouped.rearrange("p (m u) -> p m u", u=2), turned[:].rearrange("p u m -> p m u")
            )
            v_codes = keep.tile([P, P], U32, name="v_codes%d" % t, align_bytes=64)
            v_scales = keep.tile([P, P], U8, name="v_scales%d" % t, align_bytes=64)
            nc.vector.quantize_mx(v_codes[:].bitcast(FP8X4), v_scales[:], grouped.bitcast(BF16))
            for h in range(2):
                q_cols = slice(h * HALF, (h + 1) * HALF)
                nc.tensor.matmul_mx(
                    sums[h][:, t, :],
                    lhsT=v_codes[:].bitcast(FP8X4),
                    lhsT_scale=v_scales[:],
                    rhs=w_codes[:, q_cols].bitcast(FP8X4),
                    rhs_scale=w_scales[:, q_cols],
                    start=True,
                    stop=True,
                )
            if t == 1:
                early = held[:, 2 * P :].rearrange("p (t q) -> p t q", t=2)
                for h in range(2):
                    nc.scalar.copy(early[:, :, h * HALF : (h + 1) * HALF], sums[h][:, :2, :])
                nc.sync.dma_start(out_by_pair[0], early)

        for h, engine_copy in ((1, nc.scalar.copy), (0, nc.vector.tensor_copy)):
            engine_copy(
                rounded[:, h * HALF * PACK : (h + 1) * HALF * PACK].rearrange("p (q t) -> p q t", t=PACK),
                sums[h][:].rearrange("p t q -> p q t"),
            )
        for h in (1, 0):
            q_cols = slice(h * HALF, (h + 1) * HALF)
            nc.vector.quantize_mx(
                out_codes[:, q_cols].bitcast(FP8X4),
                out_scales[:, q_cols],
                rounded[:, h * HALF * PACK : (h + 1) * HALF * PACK],
            )
        late = keep.tile([P, 2, Q], F32, name="late")
        for h in (1, 0):
            nc.scalar.copy(late[:, :, h * HALF : (h + 1) * HALF], sums[h][:, 2:, :])
        nc.scalar.dma_start(out_by_pair[1], late[:])

        nc.sync.dma_start(out_1[0].rearrange("p q t -> p (q t)").bitcast(I32), out_codes[:].bitcast(I32))
        for g in range(QUADS):
            (nc.sync if g < 2 else nc.scalar).dma_start(
                out_2[0, 4 * g : 4 * g + 4, :].bitcast(I32), out_scales[32 * g : 32 * g + 4, :].bitcast(I32)
            )
